import numpy as np
CORES = [0,1,2,3,4,5,6,7,8,9,10,11,12,13,14,15,16,17,18,19,20,21,22,23,24,25,26,27,28,29,30,31,32,33,34,35,36,37,38,39,40,41,42,43,44,45,46,47,48,49,50,51,52,53,54,55,56,57,58,59,60,61,62,63,64,65,66,67,68,69,70,71,72,73,74,75,76,77,78,79,80,81,82,83,84,85,86,87,88,89,90,91,92,93,94,95,96,97,98,99,100,101,102,103,104,105,106,107,108,109,110,111,112,113,114,115,116,117,118,119,120,121,122,123,124,125,126,127,168,169,170,171,172,173,174,175]
N = 136
def setup_inputs(rng):
    return {"x": rng.standard_normal((N, 128, 1024), dtype=np.float32)}
def reference(x):
    s = x.sum(axis=0, dtype=np.float64).astype(x.dtype)
    return {"y": np.broadcast_to(s, (N,) + s.shape)}

@@ -1,0 +1,131 @@
+from concourse.bass import DstId, RemoteDMATransfer
+
+BLOCK, PIECE = 128, 16
+A = (2, 3, 6, 7)
+B = (0, 1, 4, 5)
+X_HOST, X_CHIP, RELAY_CHIP = 1, 5, 4
+
+SCRATCH = {
+    "xs": ("sbuf", [128, 8 * BLOCK], "float32"),
+    "chipl": ("sbuf", [128, 7 * BLOCK], "float32"),
+    "matel": ("sbuf", [128, BLOCK], "float32"),
+    "planel": ("sbuf", [128, 8 * PIECE], "float32"),
+    "res": ("sbuf", [128, 8 * BLOCK], "float32"),
+}
+SEMAPHORES = ["loaded", "chip", "mate", "plane", "piece", "block", "final", "sent", "stored"]
+
+OFF_CHIP = 0x00FF
+UPPER = 0xFF00
+ALL = 0xFFFF
+
+
+def world(host, chip, k):
+    return host * 128 + chip * 8 + k
+
+
+def engines(mask):
+    return bin(mask).count("1")
+
+
+def rank_program(g, core, T, topo):
+    host, chip, k = topo.host(core), topo.chip(core), core % 8
+    on_x = host == X_HOST and chip == X_CHIP
+    relay = host == X_HOST and chip == RELAY_CHIP and k in A
+    if not (host == 0 or on_x or relay):
+        return
+    sem = T.sem
+    sent = [0]
+
+    def transfer(mask, remote_sem, srcs, dsts):
+        ids = []
+        for d, ap in dsts:
+            rid, pid = topo.addr(d, core)
+            ids.append(DstId(rid=rid, pnc=pid))
+        sent[0] += engines(mask)
+        return RemoteDMATransfer(dst_ids=ids, dma_engine_mask=mask, remote_sem=remote_sem, srcs=list(srcs),
+                                 dsts=[ap for d, ap in dsts], alu_op=1 if len(srcs) > 1 else 0)
+
+    def issue(transfers):
+        g.remote_dma_fused(transfers, local_sem=sem.sent)
+
+    def cols(h, t, q=None):
+        lo = (4 * h + t) * BLOCK
+        return slice(lo, lo + BLOCK) if q is None else slice(lo + q * PIECE, lo + (q + 1) * PIECE)
+
+    if relay:
+        t = A.index(k)
+        g.wait_ge(sem.piece, 8 * engines(OFF_CHIP))
+        issue([transfer(OFF_CHIP, sem.block, [T.matel[:, :]], [(world(X_HOST, X_CHIP, A[t]), T.res[:, cols(0, t)])])])
+        g.wait_ge(sem.sent, sent[0])
+        return
+
+    p, q = chip % 2, chip // 2
+    is_a = k in A
+    t = A.index(k) if is_a else B.index(k)
+    others = [j for j in range(8) if j != k]
+
+    def half_of(j):
+        return 1 - p if j in A else p
+
+    def index_of(j):
+        return A.index(j) if j in A else B.index(j)
+
+    mine = half_of(k)
+
+    def copies(part):
+        lo = (4 * mine + t) * BLOCK
+        own = T.xs[:, lo + part.start:lo + part.stop]
+        return [own] + [T.chipl[:, s * BLOCK + part.start:s * BLOCK + part.stop] for s in range(7)]
+
+    def piece(i):
+        return slice(i * PIECE, (i + 1) * PIECE)
+
+    def broadcast(h, mask):
+        return transfer(mask, sem.final, [T.res[:, cols(h, t)]],
+                        [(world(host, chip, j), T.res[:, cols(h, t)]) for j in others])
+
+    g.dma_start(T.xs[:, :], T.x[:, :]).then_inc(sem.loaded, 16)
+    g.wait_ge(sem.loaded, 16)
+
+    issue([transfer(3 << (2 * n), sem.chip, [T.xs[:, cols(half_of(j), index_of(j))]],
+                    [(world(host, chip, j), T.chipl[:, (k - (k > j)) * BLOCK:(k - (k > j) + 1) * BLOCK])])
+           for n, j in enumerate(others)])
+    g.wait_ge(sem.chip, 7 * 2)
+
+    if on_x:
+        issue([transfer(1 << i, sem.plane, copies(piece(i)),
+                        [(world(0, 2 * i + mine, B[t]), T.planel[:, 7 * PIECE:8 * PIECE])]) for i in range(8)])
+        if is_a:
+            g.wait_ge(sem.block, engines(OFF_CHIP))
+        else:
+            g.wait_ge(sem.piece, 8 * engines(OFF_CHIP))
+        issue([broadcast(mine, ALL)])
+        g.wait_ge(sem.final, 7 * engines(ALL))
+    elif is_a:
+        mate_b = world(0, chip ^ 1, B[t])
+        issue([transfer(OFF_CHIP, sem.mate, copies(slice(0, BLOCK)), [(mate_b, T.matel[:, :])])])
+        g.wait_ge(sem.piece, 8 * engines(OFF_CHIP))
+        issue([transfer(OFF_CHIP, sem.block, [T.res[:, cols(p, t)]], [(mate_b, T.res[:, cols(p, t)])]),
+               broadcast(p, UPPER)])
+        g.wait_ge(sem.final, 3 * engines(UPPER) + 4 * engines(ALL))
+    else:
+        g.wait_ge(sem.mate, engines(OFF_CHIP))
+        peers = [i for i in range(8) if i != q]
+        issue([transfer(1 << n, sem.plane, copies(piece(i)) + [T.matel[:, piece(i)]],
+                        [(world(0, 2 * i + p, k), T.planel[:, piece(q - (q > i))])]) for n, i in enumerate(peers)])
+        g.wait_ge(sem.plane, 8)
+        place = T.res[:, cols(p, t, q)]
+        dsts = [(world(0, 2 * i + p, A[t]), place) for i in range(8)]
+        if p == X_CHIP % 2:
+            dsts.append((world(X_HOST, X_CHIP, B[t]), place))
+        else:
+            dsts.append((world(X_HOST, RELAY_CHIP, A[t]), T.matel[:, piece(q)]))
+        issue([transfer(OFF_CHIP, sem.piece,
+                        copies(piece(q)) + [T.matel[:, piece(q)]] + [T.planel[:, piece(s)] for s in range(8)], dsts)])
+        g.wait_ge(sem.block, engines(OFF_CHIP))
+        issue([broadcast(1 - p, ALL)])
+        g.wait_ge(sem.final, 4 * engines(UPPER) + 3 * engines(ALL))
+
+    g.dma_start(T.y[:, :], T.res[:, :]).then_inc(sem.stored, 16)
+    g.wait_ge(sem.stored, 16)
+    g.wait_ge(sem.sent, sent[0])

@@ -1,22 +1,19 @@
 from concourse.bass import DstId, RemoteDMATransfer
 
-BLOCK, PIECE = 128, 16
+W = 32
+U = 4
 A = (2, 3, 6, 7)
 B = (0, 1, 4, 5)
 X_HOST, X_CHIP, RELAY_CHIP = 1, 5, 4
 
 SCRATCH = {
-    "xs": ("sbuf", [128, 8 * BLOCK], "float32"),
-    "chipl": ("sbuf", [128, 7 * BLOCK], "float32"),
-    "matel": ("sbuf", [128, BLOCK], "float32"),
-    "planel": ("sbuf", [128, 8 * PIECE], "float32"),
-    "res": ("sbuf", [128, 8 * BLOCK], "float32"),
+    "xs": ("dram", [8 * U, 128, W], "float32"),
+    "chipl": ("dram", [7 * U, 128, W], "float32"),
+    "pair": ("dram", [2 * U, 128, W], "float32"),
+    "sums": ("dram", [9, 128, W], "float32"),
+    "res": ("dram", [8 * U, 128, W], "float32"),
 }
-SEMAPHORES = ["loaded", "chip", "mate", "plane", "piece", "block", "final", "sent", "stored"]
-
-OFF_CHIP = 0x00FF
-UPPER = 0xFF00
-ALL = 0xFFFF
+SEMAPHORES = ["loaded", "chip", "pair", "sums", "unit", "block", "final", "sent", "stored"]
 
 
 def world(host, chip, k):
@@ -25,6 +22,10 @@ def world(host, chip, k):
 
 def engines(mask):
     return bin(mask).count("1")
+
+
+def idx(b, u):
+    return 8 * u + b
 
 
 def rank_program(g, core, T, topo):
@@ -48,84 +49,71 @@ def rank_program(g, core, T, topo):
     def issue(transfers):
         g.remote_dma_fused(transfers, local_sem=sem.sent)
 
-    def cols(h, t, q=None):
-        lo = (4 * h + t) * BLOCK
-        return slice(lo, lo + BLOCK) if q is None else slice(lo + q * PIECE, lo + (q + 1) * PIECE)
-
-    if relay:
-        t = A.index(k)
-        g.wait_ge(sem.piece, 8 * engines(OFF_CHIP))
-        issue([transfer(OFF_CHIP, sem.block, [T.matel[:, :]], [(world(X_HOST, X_CHIP, A[t]), T.res[:, cols(0, t)])])])
-        g.wait_ge(sem.sent, sent[0])
-        return
-
     p, q = chip % 2, chip // 2
     is_a = k in A
     t = A.index(k) if is_a else B.index(k)
+
+    if relay:
+        g.wait_ge(sem.unit, U * 8)
+        issue([transfer(3 << (2 * u), sem.block, [T.res[idx(t, u)]], [(world(X_HOST, X_CHIP, A[t]), T.res[idx(t, u)])])
+               for u in range(U)])
+        g.wait_ge(sem.sent, sent[0])
+        return
+
     others = [j for j in range(8) if j != k]
 
-    def half_of(j):
-        return 1 - p if j in A else p
+    def block_of(j):
+        return 4 * (1 - p) + A.index(j) if j in A else 4 * p + B.index(j)
 
-    def index_of(j):
-        return A.index(j) if j in A else B.index(j)
+    mine = block_of(k)
 
-    mine = half_of(k)
+    def copies(u):
+        return [T.xs[idx(mine, u)]] + [T.chipl[7 * u + s] for s in range(7)]
 
-    def copies(part):
-        lo = (4 * mine + t) * BLOCK
-        own = T.xs[:, lo + part.start:lo + part.stop]
-        return [own] + [T.chipl[:, s * BLOCK + part.start:s * BLOCK + part.stop] for s in range(7)]
+    def owner(b, u):
+        return world(0, 2 * (2 * u + b % 2) + b // 4, B[b % 4])
 
-    def piece(i):
-        return slice(i * PIECE, (i + 1) * PIECE)
+    def broadcast(b, u, mask):
+        return transfer(mask, sem.final, [T.res[idx(b, u)]], [(world(host, chip, j), T.res[idx(b, u)]) for j in others])
 
-    def broadcast(h, mask):
-        return transfer(mask, sem.final, [T.res[:, cols(h, t)]],
-                        [(world(host, chip, j), T.res[:, cols(h, t)]) for j in others])
-
-    g.dma_start(T.xs[:, :], T.x[:, :]).then_inc(sem.loaded, 16)
+    g.dma_start(T.xs[:], T.x[:, :]).then_inc(sem.loaded, 16)
     g.wait_ge(sem.loaded, 16)
 
-    issue([transfer(3 << (2 * n), sem.chip, [T.xs[:, cols(half_of(j), index_of(j))]],
-                    [(world(host, chip, j), T.chipl[:, (k - (k > j)) * BLOCK:(k - (k > j) + 1) * BLOCK])])
-           for n, j in enumerate(others)])
-    g.wait_ge(sem.chip, 7 * 2)
+    for u in range(U):
+        issue([transfer(3 << (2 * n), sem.chip, [T.xs[idx(block_of(j), u)]],
+                        [(world(host, chip, j), T.chipl[7 * u + k - (k > j)])]) for n, j in enumerate(others)])
+    g.wait_ge(sem.chip, 7 * U * 2)
 
     if on_x:
-        issue([transfer(1 << i, sem.plane, copies(piece(i)),
-                        [(world(0, 2 * i + mine, B[t]), T.planel[:, 7 * PIECE:8 * PIECE])]) for i in range(8)])
+        issue([transfer(3 << (2 * u), sem.sums, copies(u), [(owner(mine, u), T.sums[8])]) for u in range(U)])
         if is_a:
-            g.wait_ge(sem.block, engines(OFF_CHIP))
+            g.wait_ge(sem.block, U * 2)
         else:
-            g.wait_ge(sem.piece, 8 * engines(OFF_CHIP))
-        issue([broadcast(mine, ALL)])
-        g.wait_ge(sem.final, 7 * engines(ALL))
+            g.wait_ge(sem.unit, U * 8)
+        issue([broadcast(mine, u, 0xF << (4 * u)) for u in range(U)])
+        g.wait_ge(sem.final, 7 * U * 4)
     elif is_a:
-        mate_b = world(0, chip ^ 1, B[t])
-        issue([transfer(OFF_CHIP, sem.mate, copies(slice(0, BLOCK)), [(mate_b, T.matel[:, :])])])
-        g.wait_ge(sem.piece, 8 * engines(OFF_CHIP))
-        issue([transfer(OFF_CHIP, sem.block, [T.res[:, cols(p, t)]], [(mate_b, T.res[:, cols(p, t)])]),
-               broadcast(p, UPPER)])
-        g.wait_ge(sem.final, 3 * engines(UPPER) + 4 * engines(ALL))
+        own = 4 * p + t
+        issue([transfer(3 << (2 * u), sem.pair, copies(u), [(world(0, chip ^ 1, k), T.pair[2 * u + 1])]) for u in range(U)])
+        g.wait_ge(sem.pair, U * 2 + U * 4)
+        issue([transfer(3 << (2 * u), sem.sums, [T.pair[2 * u], T.pair[2 * u + 1]], [(owner(own, u), T.sums[q])])
+               for u in range(U)])
+        g.wait_ge(sem.unit, U * 8)
+        issue([transfer(3 << (2 * u), sem.block, [T.res[idx(own, u)]], [(world(0, chip ^ 1, B[t]), T.res[idx(own, u)])])
+               for u in range(U)] + [broadcast(own, u, 3 << (8 + 2 * u)) for u in range(U)])
+        g.wait_ge(sem.final, 3 * U * 2 + 4 * U * 4)
     else:
-        g.wait_ge(sem.mate, engines(OFF_CHIP))
-        peers = [i for i in range(8) if i != q]
-        issue([transfer(1 << n, sem.plane, copies(piece(i)) + [T.matel[:, piece(i)]],
-                        [(world(0, 2 * i + p, k), T.planel[:, piece(q - (q > i))])]) for n, i in enumerate(peers)])
-        g.wait_ge(sem.plane, 8)
-        place = T.res[:, cols(p, t, q)]
-        dsts = [(world(0, 2 * i + p, A[t]), place) for i in range(8)]
-        if p == X_CHIP % 2:
-            dsts.append((world(X_HOST, X_CHIP, B[t]), place))
-        else:
-            dsts.append((world(X_HOST, RELAY_CHIP, A[t]), T.matel[:, piece(q)]))
-        issue([transfer(OFF_CHIP, sem.piece,
-                        copies(piece(q)) + [T.matel[:, piece(q)]] + [T.planel[:, piece(s)] for s in range(8)], dsts)])
-        g.wait_ge(sem.block, engines(OFF_CHIP))
-        issue([broadcast(1 - p, ALL)])
-        g.wait_ge(sem.final, 4 * engines(UPPER) + 3 * engines(ALL))
+        issue([transfer(0xF << (4 * u), sem.pair, copies(u), [(world(0, chip, A[t]), T.pair[2 * u])]) for u in range(U)])
+        if t % 2 == q % 2:
+            g.wait_ge(sem.sums, 9 * 2)
+            place = T.res[idx(mine, q // 2)]
+            dsts = [(world(0, 2 * ((q + 1 + r) % 8) + p, A[t]), place) for r in range(8)]
+            dsts.insert(q, (world(X_HOST, X_CHIP, B[t]) if p == X_CHIP % 2 else world(X_HOST, RELAY_CHIP, A[t]), place))
+            issue([transfer(0xFF, sem.unit, [T.sums[s] for s in range(9)], dsts)])
+        g.wait_ge(sem.block, U * 2)
+        issue([broadcast(4 * (1 - p) + t, u, 0xF << (4 * u)) for u in range(U)])
+        g.wait_ge(sem.final, 4 * U * 2 + 3 * U * 4)
 
-    g.dma_start(T.y[:, :], T.res[:, :]).then_inc(sem.stored, 16)
+    g.dma_start(T.y[:, :], T.res[:]).then_inc(sem.stored, 16)
     g.wait_ge(sem.stored, 16)
     g.wait_ge(sem.sent, sent[0])

@@ -13,7 +13,11 @@ SCRATCH = {
     "sums": ("dram", [9, 128, W], "float32"),
     "res": ("dram", [8 * U, 128, W], "float32"),
 }
-SEMAPHORES = ["loaded", "chip", "pair", "sums", "unit", "block", "final", "sent", "stored"]
+SEMAPHORES = ["loaded", "sums", "sent", "stored",
+              "chip0", "chip1", "chip2", "chip3", "pair0", "pair1", "pair2", "pair3", "unit0", "unit1", "unit2", "unit3",
+              "block0", "block1", "block2", "block3", "fin0", "fin1", "fin2", "fin3"]
+
+LOW, HIGH, ALL = 0x00FF, 0xFF00, 0xFFFF
 
 
 def world(host, chip, k):
@@ -35,6 +39,11 @@ def rank_program(g, core, T, topo):
     if not (host == 0 or on_x or relay):
         return
     sem = T.sem
+    s_chip = [sem.chip0, sem.chip1, sem.chip2, sem.chip3]
+    s_pair = [sem.pair0, sem.pair1, sem.pair2, sem.pair3]
+    s_unit = [sem.unit0, sem.unit1, sem.unit2, sem.unit3]
+    s_block = [sem.block0, sem.block1, sem.block2, sem.block3]
+    s_fin = [sem.fin0, sem.fin1, sem.fin2, sem.fin3]
     sent = [0]
 
     def transfer(mask, remote_sem, srcs, dsts):
@@ -52,11 +61,14 @@ def rank_program(g, core, T, topo):
     p, q = chip % 2, chip // 2
     is_a = k in A
     t = A.index(k) if is_a else B.index(k)
+    down = [(q // 2 + 1 + r) % U for r in range(U)]
+    place9 = 8 if host == X_HOST else q
+    up = [(place9 // 2 - (0 if place9 % 2 else 1) - w) % U for w in range(U)]
 
     if relay:
-        g.wait_ge(sem.unit, U * 8)
-        issue([transfer(3 << (2 * u), sem.block, [T.res[idx(t, u)]], [(world(X_HOST, X_CHIP, A[t]), T.res[idx(t, u)])])
-               for u in range(U)])
+        for u in up:
+            g.wait_ge(s_unit[u], 8)
+            issue([transfer(LOW, s_block[u], [T.res[idx(t, u)]], [(world(X_HOST, X_CHIP, A[t]), T.res[idx(t, u)])])])
         g.wait_ge(sem.sent, sent[0])
         return
 
@@ -74,46 +86,56 @@ def rank_program(g, core, T, topo):
         return world(0, 2 * (2 * u + b % 2) + b // 4, B[b % 4])
 
     def broadcast(b, u, mask):
-        return transfer(mask, sem.final, [T.res[idx(b, u)]], [(world(host, chip, j), T.res[idx(b, u)]) for j in others])
+        return transfer(mask, s_fin[u], [T.res[idx(b, u)]], [(world(host, chip, j), T.res[idx(b, u)]) for j in others])
 
     g.dma_start(T.xs[:], T.x[:, :]).then_inc(sem.loaded, 16)
     g.wait_ge(sem.loaded, 16)
 
-    for u in range(U):
-        issue([transfer(3 << (2 * n), sem.chip, [T.xs[idx(block_of(j), u)]],
+    for u in down:
+        issue([transfer(3 << (2 * n), s_chip[u], [T.xs[idx(block_of(j), u)]],
                         [(world(host, chip, j), T.chipl[7 * u + k - (k > j)])]) for n, j in enumerate(others)])
-    g.wait_ge(sem.chip, 7 * U * 2)
 
     if on_x:
-        issue([transfer(3 << (2 * u), sem.sums, copies(u), [(owner(mine, u), T.sums[8])]) for u in range(U)])
-        if is_a:
-            g.wait_ge(sem.block, U * 2)
-        else:
-            g.wait_ge(sem.unit, U * 8)
-        issue([broadcast(mine, u, 0xF << (4 * u)) for u in range(U)])
-        g.wait_ge(sem.final, 7 * U * 4)
+        for u in down:
+            g.wait_ge(s_chip[u], 7 * 2)
+            issue([transfer(LOW, sem.sums, copies(u), [(owner(mine, u), T.sums[8])])])
+        for u in up:
+            g.wait_ge((s_block if is_a else s_unit)[u], 8)
+            issue([broadcast(mine, u, ALL)])
+        arrive = 7 * 16
     elif is_a:
         own = 4 * p + t
-        issue([transfer(3 << (2 * u), sem.pair, copies(u), [(world(0, chip ^ 1, k), T.pair[2 * u + 1])]) for u in range(U)])
-        g.wait_ge(sem.pair, U * 2 + U * 4)
-        issue([transfer(3 << (2 * u), sem.sums, [T.pair[2 * u], T.pair[2 * u + 1]], [(owner(own, u), T.sums[q])])
-               for u in range(U)])
-        g.wait_ge(sem.unit, U * 8)
-        issue([transfer(3 << (2 * u), sem.block, [T.res[idx(own, u)]], [(world(0, chip ^ 1, B[t]), T.res[idx(own, u)])])
-               for u in range(U)] + [broadcast(own, u, 3 << (8 + 2 * u)) for u in range(U)])
-        g.wait_ge(sem.final, 3 * U * 2 + 4 * U * 4)
+        for u in down:
+            g.wait_ge(s_chip[u], 7 * 2)
+            issue([transfer(LOW, s_pair[u], copies(u), [(world(0, chip ^ 1, k), T.pair[2 * u + 1])])])
+        for u in down:
+            g.wait_ge(s_pair[u], 8 + 16)
+            issue([transfer(LOW, sem.sums, [T.pair[2 * u], T.pair[2 * u + 1]], [(owner(own, u), T.sums[q])])])
+        for u in up:
+            g.wait_ge(s_unit[u], 8)
+            issue([transfer(LOW, s_block[u], [T.res[idx(own, u)]], [(world(0, chip ^ 1, B[t]), T.res[idx(own, u)])]),
+                   broadcast(own, u, HIGH)])
+        arrive = 3 * 8 + 4 * 16
     else:
-        issue([transfer(0xF << (4 * u), sem.pair, copies(u), [(world(0, chip, A[t]), T.pair[2 * u])]) for u in range(U)])
+        for u in down:
+            g.wait_ge(s_chip[u], 7 * 2)
+            issue([transfer(ALL, s_pair[u], copies(u), [(world(0, chip, A[t]), T.pair[2 * u])])])
         if t % 2 == q % 2:
-            g.wait_ge(sem.sums, 9 * 2)
-            place = T.res[idx(mine, q // 2)]
-            dsts = [(world(0, 2 * ((q + 1 + r) % 8) + p, A[t]), place) for r in range(8)]
-            dsts.insert(q, (world(X_HOST, X_CHIP, B[t]) if p == X_CHIP % 2 else world(X_HOST, RELAY_CHIP, A[t]), place))
-            issue([transfer(0xFF, sem.unit, [T.sums[s] for s in range(9)], dsts)])
-        g.wait_ge(sem.block, U * 2)
-        issue([broadcast(4 * (1 - p) + t, u, 0xF << (4 * u)) for u in range(U)])
-        g.wait_ge(sem.final, 4 * U * 2 + 3 * U * 4)
+            g.wait_ge(sem.sums, 9 * 8)
+            spot = T.res[idx(mine, q // 2)]
+            far = world(X_HOST, X_CHIP, B[t]) if p == X_CHIP % 2 else world(X_HOST, RELAY_CHIP, A[t])
+            ring = [(q + 1 + r) % 9 for r in range(8)]
+            dsts = [(far if i == 8 else world(0, 2 * i + p, A[t]), spot) for i in ring]
+            home = (world(0, chip, A[t]), spot)
+            dsts = [home] + dsts if q % 2 else dsts + [home]
+            issue([transfer(LOW, s_unit[q // 2], [T.sums[s] for s in range(9)], dsts)])
+        for u in up:
+            g.wait_ge(s_block[u], 8)
+            issue([broadcast(4 * (1 - p) + t, u, ALL)])
+        arrive = 4 * 8 + 3 * 16
 
+    for u in up:
+        g.wait_ge(s_fin[u], arrive)
     g.dma_start(T.y[:, :], T.res[:]).then_inc(sem.stored, 16)
     g.wait_ge(sem.stored, 16)
     g.wait_ge(sem.sent, sent[0])

from concourse.bass import DstId, RemoteDMATransfer

W = 32
U = 4
A = (2, 3, 6, 7)
B = (0, 1, 4, 5)
X_HOST, X_CHIP, RELAY_CHIP = 1, 5, 4

SCRATCH = {
    "xs": ("dram", [8 * U, 128, W], "float32"),
    "chipl": ("dram", [7 * U, 128, W], "float32"),
    "pair": ("dram", [2 * U, 128, W], "float32"),
    "sums": ("dram", [9, 128, W], "float32"),
    "res": ("dram", [8 * U, 128, W], "float32"),
}
SEMAPHORES = ["loaded", "sums", "sent", "stored",
              "chip0", "chip1", "chip2", "chip3", "pair0", "pair1", "pair2", "pair3", "unit0", "unit1", "unit2", "unit3",
              "block0", "block1", "block2", "block3", "fin0", "fin1", "fin2", "fin3"]

LOW, HIGH, ALL = 0x00FF, 0xFF00, 0xFFFF


def world(host, chip, k):
    return host * 128 + chip * 8 + k


def engines(mask):
    return bin(mask).count("1")


def idx(b, u):
    return 8 * u + b


def rank_program(g, core, T, topo):
    host, chip, k = topo.host(core), topo.chip(core), core % 8
    on_x = host == X_HOST and chip == X_CHIP
    relay = host == X_HOST and chip == RELAY_CHIP and k in A
    if not (host == 0 or on_x or relay):
        return
    sem = T.sem
    s_chip = [sem.chip0, sem.chip1, sem.chip2, sem.chip3]
    s_pair = [sem.pair0, sem.pair1, sem.pair2, sem.pair3]
    s_unit = [sem.unit0, sem.unit1, sem.unit2, sem.unit3]
    s_block = [sem.block0, sem.block1, sem.block2, sem.block3]
    s_fin = [sem.fin0, sem.fin1, sem.fin2, sem.fin3]
    sent = [0]

    def transfer(mask, remote_sem, srcs, dsts):
        ids = []
        for d, ap in dsts:
            rid, pid = topo.addr(d, core)
            ids.append(DstId(rid=rid, pnc=pid))
        sent[0] += engines(mask)
        return RemoteDMATransfer(dst_ids=ids, dma_engine_mask=mask, remote_sem=remote_sem, srcs=list(srcs),
                                 dsts=[ap for d, ap in dsts], alu_op=1 if len(srcs) > 1 else 0)

    def issue(transfers):
        g.remote_dma_fused(transfers, local_sem=sem.sent)

    p, q = chip % 2, chip // 2
    is_a = k in A
    t = A.index(k) if is_a else B.index(k)
    down = [(q // 2 + 1 + r) % U for r in range(U)]
    place9 = 8 if host == X_HOST else q
    up = [(place9 // 2 - (0 if place9 % 2 else 1) - w) % U for w in range(U)]

    if relay:
        for u in up:
            g.wait_ge(s_unit[u], 8)
            issue([transfer(LOW, s_block[u], [T.res[idx(t, u)]], [(world(X_HOST, X_CHIP, A[t]), T.res[idx(t, u)])])])
        g.wait_ge(sem.sent, sent[0])
        return

    others = [j for j in range(8) if j != k]

    def block_of(j):
        return 4 * (1 - p) + A.index(j) if j in A else 4 * p + B.index(j)

    mine = block_of(k)

    def copies(u):
        return [T.xs[idx(mine, u)]] + [T.chipl[7 * u + s] for s in range(7)]

    def owner(b, u):
        return world(0, 2 * (2 * u + b % 2) + b // 4, B[b % 4])

    def broadcast(b, u, mask):
        return transfer(mask, s_fin[u], [T.res[idx(b, u)]], [(world(host, chip, j), T.res[idx(b, u)]) for j in others])

    g.dma_start(T.xs[:], T.x[:, :]).then_inc(sem.loaded, 16)
    g.wait_ge(sem.loaded, 16)

    for u in down:
        issue([transfer(3 << (2 * n), s_chip[u], [T.xs[idx(block_of(j), u)]],
                        [(world(host, chip, j), T.chipl[7 * u + k - (k > j)])]) for n, j in enumerate(others)])

    if on_x:
        for u in down:
            g.wait_ge(s_chip[u], 7 * 2)
            issue([transfer(LOW, sem.sums, copies(u), [(owner(mine, u), T.sums[8])])])
        for u in up:
            g.wait_ge((s_block if is_a else s_unit)[u], 8)
            issue([broadcast(mine, u, ALL)])
        arrive = 7 * 16
    elif is_a:
        own = 4 * p + t
        for u in down:
            g.wait_ge(s_chip[u], 7 * 2)
            issue([transfer(LOW, s_pair[u], copies(u), [(world(0, chip ^ 1, k), T.pair[2 * u + 1])])])
        for u in down:
            g.wait_ge(s_pair[u], 8 + 16)
            issue([transfer(LOW, sem.sums, [T.pair[2 * u], T.pair[2 * u + 1]], [(owner(own, u), T.sums[q])])])
        for u in up:
            g.wait_ge(s_unit[u], 8)
            issue([transfer(LOW, s_block[u], [T.res[idx(own, u)]], [(world(0, chip ^ 1, B[t]), T.res[idx(own, u)])]),
                   broadcast(own, u, HIGH)])
        arrive = 3 * 8 + 4 * 16
    else:
        for u in down:
            g.wait_ge(s_chip[u], 7 * 2)
            issue([transfer(ALL, s_pair[u], copies(u), [(world(0, chip, A[t]), T.pair[2 * u])])])
        if t % 2 == q % 2:
            g.wait_ge(sem.sums, 9 * 8)
            spot = T.res[idx(mine, q // 2)]
            far = world(X_HOST, X_CHIP, B[t]) if p == X_CHIP % 2 else world(X_HOST, RELAY_CHIP, A[t])
            ring = [(q + 1 + r) % 9 for r in range(8)]
            dsts = [(far if i == 8 else world(0, 2 * i + p, A[t]), spot) for i in ring]
            home = (world(0, chip, A[t]), spot)
            dsts = [home] + dsts if q % 2 else dsts + [home]
            issue([transfer(LOW, s_unit[q // 2], [T.sums[s] for s in range(9)], dsts)])
        for u in up:
            g.wait_ge(s_block[u], 8)
            issue([broadcast(4 * (1 - p) + t, u, ALL)])
        arrive = 4 * 8 + 3 * 16

    for u in up:
        g.wait_ge(s_fin[u], arrive)
    g.dma_start(T.y[:, :], T.res[:]).then_inc(sem.stored, 16)
    g.wait_ge(sem.stored, 16)
    g.wait_ge(sem.sent, sent[0])
